import numpy as np, ml_dtypes
CORES = [242,247,114,119]
N = 4
import mx_ref
NC, G, MB = 128, 2, 3
C = np.float32(0.047)
BF = ml_dtypes.bfloat16
def cut(t, i, w=512):
    return t[:, w * i:w * i + w]
def tile(rs):
    return np.stack(rs, axis=2).reshape(128, -1).astype(BF)
def layer(w, X):
    out = []
    for i in range(G):
        for t in range(len(X)):
            p = mx_ref.matmul(mx_ref.quantize(cut(w, len(X) * i + t)), X[t])
            z = p if t == 0 else z + p
        out.append(z)
    return out
def act(Z):
    return [np.maximum(s * z, 0) * C for z in Z for s in (1, -1)]
def setup_inputs(rng):
    def f(*shape):
        return mx_ref.flush((rng.standard_normal(shape, dtype=np.float32) * np.exp2(rng.integers(-2, 3, shape[:-1] + (1,)))).astype(BF))
    return {"x": f(N, 128, 4 * NC), "w1": f(N, 128, G * 512), "w2": f(N, 128, 512), "px": f(N, 128, MB * 4 * NC), "pw": f(N, 128, G * 512)}
def setup_inputs_blocks(rng):
    d = setup_inputs(rng)
    for k in ("x", "w1", "w2", "px"): d[k] = mx_ref.spread(d[k], rng, 4)
    for k in ("pw",): d[k] = mx_ref.spread(d[k], rng, 1)
    return d
def setup_inputs_wide(rng):
    d = setup_inputs(rng)
    for k in ("x", "w1", "w2", "px"): d[k] = mx_ref.flush((d[k].astype(np.float32) * np.exp2(rng.integers(-6, 7, (N, 1, 1))).astype(np.float32)).astype(BF))
    return d
def setup_inputs_zeros(rng):
    d = setup_inputs(rng); v = d["x"].reshape(N, 128, -1, 4).copy()
    v[np.broadcast_to((rng.random((N, 1, v.shape[2], 1)) < 0.33), v.shape)] = 0
    d["x"] = v.reshape(d["x"].shape)
    return d
def reference(x, w1, w2, px, pw):
    H = [mx_ref.quantize(tile(act(layer(w1[j], [mx_ref.quantize(x[j])])))) for j in range(N)]
    y = np.zeros((N, 128, N * NC), np.float32)
    for r in range(N):
        qw = mx_ref.quantize(w2[r])
        for j in range(N):
            y[r][:, NC * j:NC * j + NC] = mx_ref.matmul(qw, H[j])
    z = np.full((N, 128, MB * G * NC), np.nan, np.float32)
    for m in range(MB):
        a = mx_ref.quantize(cut(px[N - 1], m, 4 * NC))
        for s in range(N - 1):
            a = mx_ref.quantize(tile(act(layer(pw[s], [a]))))
        Z = layer(pw[N - 1], [a])
        for i in range(G):
            z[N - 1][:, NC * (G * m + i):NC * (G * m + i) + NC] = Z[i]
    return {"y": y, "z": z}

@@ -1,0 +1,267 @@
+import numpy as np
+from concourse.bass import DstId, RemoteDMATransfer
+from concourse.mybir import dt, AluOpType, ActivationFunctionType
+
+COLS, HALF = 384, 192
+K = float(np.float32(0.047))
+
+SCRATCH = {
+    "xb": ("sbuf", [128, 512], "bfloat16"),
+    "w1b": ("sbuf", [128, 1024], "bfloat16"),
+    "w2b": ("sbuf", [128, 512], "bfloat16"),
+    "pwb": ("sbuf", [128, 1024], "bfloat16"),
+    "pxb": ("sbuf", [128, 1536], "bfloat16"),
+    "xq": ("sbuf", [128, 128], "float8_e4m3fn_x4"), "xs": ("sbuf", [128, 128], "uint8"),
+    "w1q": ("sbuf", [128, 256], "float8_e4m3fn_x4"), "w1s": ("sbuf", [128, 256], "uint8"),
+    "w2q": ("sbuf", [128, 128], "float8_e4m3fn_x4"), "w2s": ("sbuf", [128, 128], "uint8"),
+    "pwq": ("sbuf", [128, 256], "float8_e4m3fn_x4"), "pws": ("sbuf", [128, 256], "uint8"),
+    "pxq": ("sbuf", [128, COLS], "float8_e4m3fn_x4"), "pxs": ("sbuf", [128, COLS], "uint8"),
+    "owq": ("sbuf", [128, 256], "float8_e4m3fn_x4"), "ows": ("sbuf", [128, 256], "uint8"),
+    "hb": ("sbuf", [128, 512], "bfloat16"),
+    "hq": ("sbuf", [128, 512], "float8_e4m3fn_x4"), "hs": ("sbuf", [128, 512], "uint8"),
+    "cq": ("sbuf", [128, COLS], "float8_e4m3fn_x4"), "cs": ("sbuf", [128, COLS], "uint8"),
+    "t1b": ("sbuf", [128, 4 * COLS], "bfloat16"),
+    "t1q": ("sbuf", [128, COLS], "float8_e4m3fn_x4"), "t1s": ("sbuf", [128, COLS], "uint8"),
+    "t2b": ("sbuf", [128, 4 * COLS], "bfloat16"),
+    "t2q": ("sbuf", [128, COLS], "float8_e4m3fn_x4"), "t2s": ("sbuf", [128, COLS], "uint8"),
+    "yb": ("sbuf", [128, 512], "float32"),
+    "zb": ("sbuf", [128, 768], "float32"),
+    "b0": ("psum", [128, 512], "float32"), "b1": ("psum", [128, 512], "float32"),
+    "b2": ("psum", [128, 512], "float32"), "b3": ("psum", [128, 512], "float32"),
+    "b4": ("psum", [128, 512], "float32"), "b5": ("psum", [128, 512], "float32"),
+    "b6": ("psum", [128, 512], "float32"), "b7": ("psum", [128, 512], "float32"),
+}
+_LAYERS = ["h", "u", "v"]
+SEMAPHORES = (["ld_" + k for k in ("x", "w1", "w2", "pw", "px0", "px1")]
+              + ["q_" + k for k in ("x", "w1", "w2", "pw", "px0", "px1")]
+              + [p + k for k in _LAYERS for p in ("m0_", "m1_", "s_", "v_", "q_")]
+              + ["m0_y", "m1_y", "s_y", "v_y", "m0_za", "m1_za", "m0_zb", "m1_zb", "s_z0", "v_z0", "s_z1", "v_z1"]
+              + ["h_in", "w_in", "c_in", "a_in", "b_in", "sent", "c_sent", "stored"])
+
+
+def _engines(mask):
+    return [1 << k for k in range(mask.bit_length()) if mask >> k & 1]
+
+
+def _same_chip(topo, a, b):
+    return topo.host(a) == topo.host(b) and topo.chip(a) == topo.chip(b)
+
+
+def _shares(topo, src, dsts):
+    off = [d for d in dsts if not _same_chip(topo, src, d)]
+    on = [d for d in dsts if _same_chip(topo, src, d)]
+    out = {}
+    taken = 0
+    for group in (off, on):
+        if group:
+            free = _engines(topo.mask(src, group[0]) & ~taken)
+            each = 1 << ((len(free) // len(group)).bit_length() - 1)
+            for k, d in enumerate(group):
+                out[d] = sum(free[k * each:(k + 1) * each])
+            taken |= sum(free)
+    return out
+
+
+def rank_program(g, core, T, topo):
+    rank = T.rank_of(core)
+    if rank is None:
+        return
+    S, cores = T.sem, T.cores
+    n_ranks = len(cores)
+    first, mid_b, mid_a, last = 0, 1, 2, n_ranks - 1
+    A, B = (0, HALF), (HALF, COLS)
+
+    def load(queue, buf, src, lo, hi, sem):
+        queue.dma_start(buf[:, lo:hi], src[:, lo:hi]).then_inc(S[sem], 16)
+
+    def pack(q, s, b, lo, hi, ld, sem):
+        g.vector.wait_ge(S[ld], 16)
+        g.vector.quantize_mx(q[:, lo:hi], s[:, lo:hi], b[:, 4 * lo:4 * hi]).then_inc(S[sem], 1)
+
+    def layer(tag, waits, wq, ws, iq, isc, ilo, n, bank0, bank1, tb, tlo, oq, osc, olo):
+        for sem, val in waits:
+            g.tensor.wait_ge(S[sem], val)
+        for i, bank in ((0, bank0), (1, bank1)):
+            g.tensor.matmul_mx(bank[:, 0:n], wq[:, 128 * i:128 * i + 128], ws[:, 128 * i:128 * i + 128],
+                               iq[:, ilo:ilo + n], isc[:, ilo:ilo + n], True, True).then_inc(S["m%d_%s" % (i, tag)], 1)
+        lo, hi = 4 * tlo, 4 * (tlo + n)
+        g.scalar.wait_ge(S["m0_" + tag], 1)
+        g.vector.wait_ge(S["m1_" + tag], 1)
+        for b, k in ((0, K), (1, -K)):
+            g.scalar.activation(tb[:, lo + b:hi:4], bank0[:, 0:n], ActivationFunctionType.Relu,
+                                scale=k).then_inc(S["s_" + tag], 1)
+            g.vector.tensor_scalar(tb[:, lo + 2 + b:hi:4], bank1[:, 0:n], k, 0.0,
+                                   AluOpType.mult, AluOpType.max).then_inc(S["v_" + tag], 1)
+        g.vector.wait_ge(S["s_" + tag], 2)
+        g.vector.wait_ge(S["v_" + tag], 2)
+        g.vector.quantize_mx(oq[:, olo:olo + n], osc[:, olo:olo + n], tb[:, lo:hi]).then_inc(S["q_" + tag], 1)
+
+    def views(q, s, lo, hi):
+        return q[:, lo:hi].bitcast(dt.uint8), s[:, lo:hi]
+
+    def count(mask):
+        return len(_engines(mask))
+
+    def send(dst, out, in_, mask, sem, local):
+        rid, pid = topo.addr(cores[dst], core)
+        g.remote_dma(out, in_, S[sem], S[local], pid, rid, mask)
+        return count(mask)
+
+    def send_pair(dst, dq, ds, sq, ss, lo, hi, mask, sem, local):
+        n = 0
+        for out, in_ in zip(views(dq, ds, lo, hi), views(sq, ss, lo, hi)):
+            n += send(dst, out, in_, mask, sem, local)
+        return n
+
+    def send_fused(jobs, local):
+        ts = []
+        for dst, out, in_, mask, sem in jobs:
+            rid, pid = topo.addr(cores[dst], core)
+            ts.append(RemoteDMATransfer(dst_ids=[DstId(rid=rid, pnc=pid)], dma_engine_mask=mask, remote_sem=S[sem],
+                                        src=in_, dst=out))
+        g.remote_dma_fused(ts, local_sem=S[local])
+        return sum(count(j[3]) for j in jobs)
+
+    def full(src, dst):
+        return topo.mask(cores[src], cores[dst])
+
+    def h_mask(src, dst):
+        return _shares(topo, cores[src], [c for c in cores if c != cores[src]])[cores[dst]]
+
+    def send_h():
+        g.wait_ge(S.q_h, 1)
+        lo, hi = 128 * rank, 128 * rank + 128
+        n = 0
+        for v in views(T.hq, T.hs, lo, hi):
+            n += send_fused([(d, v, v, h_mask(rank, d), "h_in") for d in range(n_ranks) if d != rank], "sent")
+        return n
+
+    def make_h():
+        pack(T.xq, T.xs, T.xb, 0, 128, "ld_x", "q_x")
+        pack(T.w1q, T.w1s, T.w1b, 0, 256, "ld_w1", "q_w1")
+        layer("h", [("q_x", 1), ("q_w1", 1)], T.w1q, T.w1s, T.xq, T.xs, 0, 128, T.b0, T.b1, T.hb, 0, T.hq, T.hs, 128 * rank)
+
+    def make_y():
+        arrivals = sum(2 * count(h_mask(s, rank)) for s in range(n_ranks) if s != rank)
+        for sem, val in (("q_w2", 1), ("q_h", 1), ("h_in", arrivals)):
+            g.tensor.wait_ge(S[sem], val)
+        for k, bank in ((0, T.b6), (1, T.b7)):
+            g.tensor.matmul_mx(bank[:, 0:256], T.w2q[:, 0:128], T.w2s[:, 0:128], T.hq[:, 256 * k:256 * k + 256],
+                               T.hs[:, 256 * k:256 * k + 256], True, True).then_inc(S["m%d_y" % k], 1)
+        g.scalar.wait_ge(S.m0_y, 1)
+        g.scalar.activation(T.yb[:, 0:256], T.b6[:, 0:256], ActivationFunctionType.Copy).then_inc(S.s_y, 1)
+        g.vector.wait_ge(S.m1_y, 1)
+        g.vector.tensor_copy(T.yb[:, 256:512], T.b7[:, 0:256]).then_inc(S.v_y, 1)
+
+    def store_y():
+        g.sync.wait_ge(S.s_y, 1)
+        g.sync.wait_ge(S.v_y, 1)
+        g.sync.dma_start(T.y[:, :], T.yb[:, :]).then_inc(S.stored, 16)
+
+    hop2 = _shares(topo, cores[first], [cores[mid_a], cores[mid_b]])
+    PX = ((0, 128), (128, COLS))
+    sent = 0
+
+    if rank == last:
+        for k, (lo, hi) in enumerate(PX):
+            load(g.sync, T.pxb, T.px, 4 * lo, 4 * hi, "ld_px%d" % k)
+        load(g.sync, T.xb, T.x, 0, 512, "ld_x")
+        load(g.sync, T.w1b, T.w1, 0, 1024, "ld_w1")
+        for k, (lo, hi) in enumerate(PX):
+            pack(T.pxq, T.pxs, T.pxb, lo, hi, "ld_px%d" % k, "q_px%d" % k)
+        px_sent = 0
+        m = full(last, first)
+        for k, (lo, hi) in enumerate(PX):
+            g.wait_ge(S["q_px%d" % k], 1)
+            px_sent += send(first, T.cq[:, lo:hi].bitcast(dt.uint8), T.pxq[:, lo:hi].bitcast(dt.uint8), m, "c_in", "c_sent")
+        px_sent += send(first, T.cs[:, 0:COLS], T.pxs[:, 0:COLS], m, "c_in", "c_sent")
+        make_h()
+        sent += send_h()
+        g.sync.wait_ge(S.c_sent, px_sent)
+        load(g.sync, T.w2b, T.w2, 0, 512, "ld_w2")
+        load(g.sync, T.pwb, T.pw, 0, 1024, "ld_pw")
+        pack(T.w2q, T.w2s, T.w2b, 0, 128, "ld_w2", "q_w2")
+        pack(T.pwq, T.pws, T.pwb, 0, 256, "ld_pw", "q_pw")
+        make_y()
+        store_y()
+        g.tensor.wait_ge(S.q_pw, 1)
+        for tag, (lo, hi), sem, src, banks in (("za", A, "a_in", mid_a, (T.b2, T.b3)), ("zb", B, "b_in", mid_b, (T.b4, T.b5))):
+            g.tensor.wait_ge(S[sem], 2 * count(full(src, last)))
+            for i in (0, 1):
+                g.tensor.matmul_mx(banks[i][:, 0:HALF], T.pwq[:, 128 * i:128 * i + 128], T.pws[:, 128 * i:128 * i + 128],
+                                   T.cq[:, lo:hi], T.cs[:, lo:hi], True, True).then_inc(S["m%d_%s" % (i, tag)], 1)
+            g.scalar.wait_ge(S["m0_" + tag], 1)
+            g.vector.wait_ge(S["m1_" + tag], 1)
+            for blk in range(COLS // 128):
+                c0, c1 = max(lo, 128 * blk), min(hi, 128 * blk + 128)
+                if c0 >= c1:
+                    continue
+                done = "z0" if blk == 0 else "z1"
+                for i, bank in enumerate(banks):
+                    o = 128 * (2 * blk + i) + c0 - 128 * blk
+                    out, in_ = T.zb[:, o:o + c1 - c0], bank[:, c0 - lo:c1 - lo]
+                    if i == 0:
+                        g.scalar.activation(out, in_, ActivationFunctionType.Copy).then_inc(S["s_" + done], 1)
+                    else:
+                        g.vector.tensor_copy(out, in_).then_inc(S["v_" + done], 1)
+        g.sync.wait_ge(S.s_z0, 1)
+        g.sync.wait_ge(S.v_z0, 1)
+        g.sync.dma_start(T.z[:, 0:256], T.zb[:, 0:256]).then_inc(S.stored, 16)
+        g.sync.wait_ge(S.s_z1, 3)
+        g.sync.wait_ge(S.v_z1, 3)
+        g.sync.dma_start(T.z[:, 256:768], T.zb[:, 256:768]).then_inc(S.stored, 16)
+        g.sync.wait_ge(S.stored, 48)
+
+    elif rank == first:
+        load(g.sync, T.w1b, T.w1, 0, 1024, "ld_w1")
+        load(g.scalar, T.xb, T.x, 0, 512, "ld_x")
+        load(g.sync, T.pwb, T.pw, 0, 1024, "ld_pw")
+        load(g.scalar, T.w2b, T.w2, 0, 512, "ld_w2")
+        make_h()
+        sent += send_h()
+        pack(T.pwq, T.pws, T.pwb, 0, 256, "ld_pw", "q_pw")
+        pack(T.w2q, T.w2s, T.w2b, 0, 128, "ld_w2", "q_w2")
+        px_in = 3 * count(full(last, first))
+        for tag, (lo, hi), b0, b1 in (("u", A, T.b2, T.b3), ("v", B, T.b4, T.b5)):
+            layer(tag, [("q_pw", 1), ("c_in", px_in)], T.pwq, T.pws, T.cq, T.cs, lo, HALF, b0, b1,
+                  T.t1b, lo, T.t1q, T.t1s, lo)
+        g.wait_ge(S.q_u, 1)
+        g.wait_ge(S.q_v, 1)
+        c_sent = 0
+        va, vb = views(T.t1q, T.t1s, *A), views(T.t1q, T.t1s, *B)
+        da, db = views(T.cq, T.cs, *A), views(T.cq, T.cs, *B)
+        for k in (0, 1):
+            c_sent += send_fused([(mid_a, da[k], va[k], hop2[cores[mid_a]], "c_in"),
+                                  (mid_b, db[k], vb[k], hop2[cores[mid_b]], "c_in")], "c_sent")
+        make_y()
+        g.sync.wait_ge(S.c_sent, c_sent)
+        store_y()
+        g.sync.wait_ge(S.stored, 16)
+
+    else:
+        other = mid_a if rank == mid_b else mid_b
+        lo, hi = A if rank == mid_a else B
+        load(g.sync, T.pwb, T.pw, 0, 1024, "ld_pw")
+        load(g.scalar, T.xb, T.x, 0, 512, "ld_x")
+        load(g.sync, T.w1b, T.w1, 0, 1024, "ld_w1")
+        load(g.scalar, T.w2b, T.w2, 0, 512, "ld_w2")
+        pack(T.pwq, T.pws, T.pwb, 0, 256, "ld_pw", "q_pw")
+        g.wait_ge(S.q_pw, 1)
+        sent += send_pair(other, T.owq, T.ows, T.pwq, T.pws, 0, 256, full(rank, other), "w_in", "sent")
+        make_h()
+        sent += send_h()
+        pack(T.w2q, T.w2s, T.w2b, 0, 128, "ld_w2", "q_w2")
+        make_y()
+        store_y()
+        w_in = ("w_in", 2 * count(full(other, rank)))
+        mine, theirs = (T.pwq, T.pws, ("q_pw", 1)), (T.owq, T.ows, w_in)
+        s1, s2 = (mine, theirs) if rank < other else (theirs, mine)
+        layer("u", [s1[2], ("c_in", 2 * count(hop2[core]))], s1[0], s1[1], T.cq, T.cs, lo, HALF, T.b2, T.b3,
+              T.t1b, lo, T.t1q, T.t1s, lo)
+        layer("v", [s2[2], ("q_u", 1)], s2[0], s2[1], T.t1q, T.t1s, lo, HALF, T.b4, T.b5, T.t2b, lo, T.t2q, T.t2s, lo)
+        g.wait_ge(S.q_v, 1)
+        sent += send_pair(last, T.cq, T.cs, T.t2q, T.t2s, lo, hi, full(rank, last),
+                          "a_in" if rank == mid_a else "b_in", "sent")
+        g.sync.wait_ge(S.stored, 16)
+
+    g.wait_ge(S.sent, sent)

@@ -36,7 +36,7 @@ SEMAPHORES = (["ld_" + k for k in ("x", "w1", "w2", "pw", "px0", "px1")]
               + ["q_" + k for k in ("x", "w1", "w2", "pw", "px0", "px1")]
               + [p + k for k in _LAYERS for p in ("m0_", "m1_", "s_", "v_", "q_")]
               + ["m0_y", "m1_y", "s_y", "v_y", "m0_za", "m1_za", "m0_zb", "m1_zb", "s_z0", "v_z0", "s_z1", "v_z1"]
-              + ["h_in", "w_in", "c_in", "a_in", "b_in", "sent", "c_sent", "stored"])
+              + ["h_in", "w_in", "e_in", "l_in", "sent", "c_sent", "stored"])
 
 
 def _engines(mask):
@@ -68,8 +68,8 @@ def rank_program(g, core, T, topo):
         return
     S, cores = T.sem, T.cores
     n_ranks = len(cores)
-    first, mid_b, mid_a, last = 0, 1, 2, n_ranks - 1
-    A, B = (0, HALF), (HALF, COLS)
+    first, mid_e, mid_l, last = 0, 1, 2, n_ranks - 1
+    E, L = (0, HALF), (HALF, COLS)
 
     def load(queue, buf, src, lo, hi, sem):
         queue.dma_start(buf[:, lo:hi], src[:, lo:hi]).then_inc(S[sem], 16)
@@ -107,9 +107,9 @@ def rank_program(g, core, T, topo):
         g.remote_dma(out, in_, S[sem], S[local], pid, rid, mask)
         return count(mask)
 
-    def send_pair(dst, dq, ds, sq, ss, lo, hi, mask, sem, local):
+    def send_pair(dst, dq, ds, sq, ss, lo, hi, masks, sem, local):
         n = 0
-        for out, in_ in zip(views(dq, ds, lo, hi), views(sq, ss, lo, hi)):
+        for out, in_, mask in zip(views(dq, ds, lo, hi), views(sq, ss, lo, hi), masks):
             n += send(dst, out, in_, mask, sem, local)
         return n
 
@@ -124,6 +124,12 @@ def rank_program(g, core, T, topo):
 
     def full(src, dst):
         return topo.mask(cores[src], cores[dst])
+
+    def both(src, dst):
+        return full(src, dst), full(src, dst)
+
+    def total(masks):
+        return sum(count(m) for m in masks)
 
     def h_mask(src, dst):
         return _shares(topo, cores[src], [c for c in cores if c != cores[src]])[cores[dst]]
@@ -158,8 +164,10 @@ def rank_program(g, core, T, topo):
         g.sync.wait_ge(S.v_y, 1)
         g.sync.dma_start(T.y[:, :], T.yb[:, :]).then_inc(S.stored, 16)
 
-    hop2 = _shares(topo, cores[first], [cores[mid_a], cores[mid_b]])
-    PX = ((0, 128), (128, COLS))
+    e_masks = full(first, mid_e), full(first, mid_e) & ~full(first, mid_l)
+    l_masks = both(first, mid_l)
+    PX = (E, L)
+    m_px = full(last, first)
     sent = 0
 
     if rank == last:
@@ -169,12 +177,13 @@ def rank_program(g, core, T, topo):
         load(g.sync, T.w1b, T.w1, 0, 1024, "ld_w1")
         for k, (lo, hi) in enumerate(PX):
             pack(T.pxq, T.pxs, T.pxb, lo, hi, "ld_px%d" % k, "q_px%d" % k)
-        px_sent = 0
-        m = full(last, first)
-        for k, (lo, hi) in enumerate(PX):
-            g.wait_ge(S["q_px%d" % k], 1)
-            px_sent += send(first, T.cq[:, lo:hi].bitcast(dt.uint8), T.pxq[:, lo:hi].bitcast(dt.uint8), m, "c_in", "c_sent")
-        px_sent += send(first, T.cs[:, 0:COLS], T.pxs[:, 0:COLS], m, "c_in", "c_sent")
+        cd, cs = T.cq[:, E[0]:E[1]].bitcast(dt.uint8), T.pxq[:, E[0]:E[1]].bitcast(dt.uint8)
+        g.wait_ge(S.q_px0, 1)
+        px_sent = send(first, cd, cs, m_px, "e_in", "c_sent")
+        g.wait_ge(S.q_px1, 1)
+        px_sent += send(first, T.cs[:, 0:COLS], T.pxs[:, 0:COLS], m_px, "e_in", "c_sent")
+        cd, cs = T.cq[:, L[0]:L[1]].bitcast(dt.uint8), T.pxq[:, L[0]:L[1]].bitcast(dt.uint8)
+        px_sent += send(first, cd, cs, m_px, "l_in", "c_sent")
         make_h()
         sent += send_h()
         g.sync.wait_ge(S.c_sent, px_sent)
@@ -185,8 +194,8 @@ def rank_program(g, core, T, topo):
         make_y()
         store_y()
         g.tensor.wait_ge(S.q_pw, 1)
-        for tag, (lo, hi), sem, src, banks in (("za", A, "a_in", mid_a, (T.b2, T.b3)), ("zb", B, "b_in", mid_b, (T.b4, T.b5))):
-            g.tensor.wait_ge(S[sem], 2 * count(full(src, last)))
+        for tag, (lo, hi), sem, src, banks in (("za", E, "e_in", mid_e, (T.b2, T.b3)), ("zb", L, "l_in", mid_l, (T.b4, T.b5))):
+            g.tensor.wait_ge(S[sem], total(both(src, last)))
             for i in (0, 1):
                 g.tensor.matmul_mx(banks[i][:, 0:HALF], T.pwq[:, 128 * i:128 * i + 128], T.pws[:, 128 * i:128 * i + 128],
                                    T.cq[:, lo:hi], T.cs[:, lo:hi], True, True).then_inc(S["m%d_%s" % (i, tag)], 1)
@@ -221,47 +230,43 @@ def rank_program(g, core, T, topo):
         sent += send_h()
         pack(T.pwq, T.pws, T.pwb, 0, 256, "ld_pw", "q_pw")
         pack(T.w2q, T.w2s, T.w2b, 0, 128, "ld_w2", "q_w2")
-        px_in = 3 * count(full(last, first))
-        for tag, (lo, hi), b0, b1 in (("u", A, T.b2, T.b3), ("v", B, T.b4, T.b5)):
-            layer(tag, [("q_pw", 1), ("c_in", px_in)], T.pwq, T.pws, T.cq, T.cs, lo, HALF, b0, b1,
-                  T.t1b, lo, T.t1q, T.t1s, lo)
+        layer("u", [("q_pw", 1), ("e_in", 2 * count(m_px))], T.pwq, T.pws, T.cq, T.cs, E[0], HALF, T.b2, T.b3,
+              T.t1b, E[0], T.t1q, T.t1s, E[0])
+        layer("v", [("l_in", count(m_px))], T.pwq, T.pws, T.cq, T.cs, L[0], HALF, T.b4, T.b5,
+              T.t1b, L[0], T.t1q, T.t1s, L[0])
         g.wait_ge(S.q_u, 1)
+        c_sent = send_pair(mid_e, T.cq, T.cs, T.t1q, T.t1s, E[0], E[1], e_masks, "e_in", "c_sent")
         g.wait_ge(S.q_v, 1)
-        c_sent = 0
-        va, vb = views(T.t1q, T.t1s, *A), views(T.t1q, T.t1s, *B)
-        da, db = views(T.cq, T.cs, *A), views(T.cq, T.cs, *B)
-        for k in (0, 1):
-            c_sent += send_fused([(mid_a, da[k], va[k], hop2[cores[mid_a]], "c_in"),
-                                  (mid_b, db[k], vb[k], hop2[cores[mid_b]], "c_in")], "c_sent")
+        c_sent += send_pair(mid_l, T.cq, T.cs, T.t1q, T.t1s, L[0], L[1], l_masks, "l_in", "c_sent")
         make_y()
         g.sync.wait_ge(S.c_sent, c_sent)
         store_y()
         g.sync.wait_ge(S.stored, 16)
 
     else:
-        other = mid_a if rank == mid_b else mid_b
-        lo, hi = A if rank == mid_a else B
+        other = mid_l if rank == mid_e else mid_e
+        (lo, hi), c_in, masks = (E, "e_in", e_masks) if rank == mid_e else (L, "l_in", l_masks)
         load(g.sync, T.pwb, T.pw, 0, 1024, "ld_pw")
         load(g.scalar, T.xb, T.x, 0, 512, "ld_x")
         load(g.sync, T.w1b, T.w1, 0, 1024, "ld_w1")
         load(g.scalar, T.w2b, T.w2, 0, 512, "ld_w2")
         pack(T.pwq, T.pws, T.pwb, 0, 256, "ld_pw", "q_pw")
         g.wait_ge(S.q_pw, 1)
-        sent += send_pair(other, T.owq, T.ows, T.pwq, T.pws, 0, 256, full(rank, other), "w_in", "sent")
+        sent += send_pair(other, T.owq, T.ows, T.pwq, T.pws, 0, 256, both(rank, other), "w_in", "sent")
         make_h()
         sent += send_h()
         pack(T.w2q, T.w2s, T.w2b, 0, 128, "ld_w2", "q_w2")
-        make_y()
-        store_y()
-        w_in = ("w_in", 2 * count(full(other, rank)))
+        w_in = ("w_in", total(both(other, rank)))
         mine, theirs = (T.pwq, T.pws, ("q_pw", 1)), (T.owq, T.ows, w_in)
         s1, s2 = (mine, theirs) if rank < other else (theirs, mine)
-        layer("u", [s1[2], ("c_in", 2 * count(hop2[core]))], s1[0], s1[1], T.cq, T.cs, lo, HALF, T.b2, T.b3,
+        layer("u", [s1[2], (c_in, total(masks))], s1[0], s1[1], T.cq, T.cs, lo, HALF, T.b2, T.b3,
               T.t1b, lo, T.t1q, T.t1s, lo)
         layer("v", [s2[2], ("q_u", 1)], s2[0], s2[1], T.t1q, T.t1s, lo, HALF, T.b4, T.b5, T.t2b, lo, T.t2q, T.t2s, lo)
         g.wait_ge(S.q_v, 1)
-        sent += send_pair(last, T.cq, T.cs, T.t2q, T.t2s, lo, hi, full(rank, last),
-                          "a_in" if rank == mid_a else "b_in", "sent")
+        c_sent = send_pair(last, T.cq, T.cs, T.t2q, T.t2s, lo, hi, both(rank, last), c_in, "c_sent")
+        make_y()
+        g.sync.wait_ge(S.c_sent, c_sent)
+        store_y()
         g.sync.wait_ge(S.stored, 16)
 
     g.wait_ge(S.sent, sent)

import numpy as np
from concourse.bass import DstId, RemoteDMATransfer
from concourse.mybir import dt, AluOpType, ActivationFunctionType

COLS, HALF = 384, 192
K = float(np.float32(0.047))

SCRATCH = {
    "xb": ("sbuf", [128, 512], "bfloat16"),
    "w1b": ("sbuf", [128, 1024], "bfloat16"),
    "w2b": ("sbuf", [128, 512], "bfloat16"),
    "pwb": ("sbuf", [128, 1024], "bfloat16"),
    "pxb": ("sbuf", [128, 1536], "bfloat16"),
    "xq": ("sbuf", [128, 128], "float8_e4m3fn_x4"), "xs": ("sbuf", [128, 128], "uint8"),
    "w1q": ("sbuf", [128, 256], "float8_e4m3fn_x4"), "w1s": ("sbuf", [128, 256], "uint8"),
    "w2q": ("sbuf", [128, 128], "float8_e4m3fn_x4"), "w2s": ("sbuf", [128, 128], "uint8"),
    "pwq": ("sbuf", [128, 256], "float8_e4m3fn_x4"), "pws": ("sbuf", [128, 256], "uint8"),
    "pxq": ("sbuf", [128, COLS], "float8_e4m3fn_x4"), "pxs": ("sbuf", [128, COLS], "uint8"),
    "owq": ("sbuf", [128, 256], "float8_e4m3fn_x4"), "ows": ("sbuf", [128, 256], "uint8"),
    "hb": ("sbuf", [128, 512], "bfloat16"),
    "hq": ("sbuf", [128, 512], "float8_e4m3fn_x4"), "hs": ("sbuf", [128, 512], "uint8"),
    "cq": ("sbuf", [128, COLS], "float8_e4m3fn_x4"), "cs": ("sbuf", [128, COLS], "uint8"),
    "t1b": ("sbuf", [128, 4 * COLS], "bfloat16"),
    "t1q": ("sbuf", [128, COLS], "float8_e4m3fn_x4"), "t1s": ("sbuf", [128, COLS], "uint8"),
    "t2b": ("sbuf", [128, 4 * COLS], "bfloat16"),
    "t2q": ("sbuf", [128, COLS], "float8_e4m3fn_x4"), "t2s": ("sbuf", [128, COLS], "uint8"),
    "yb": ("sbuf", [128, 512], "float32"),
    "zb": ("sbuf", [128, 768], "float32"),
    "b0": ("psum", [128, 512], "float32"), "b1": ("psum", [128, 512], "float32"),
    "b2": ("psum", [128, 512], "float32"), "b3": ("psum", [128, 512], "float32"),
    "b4": ("psum", [128, 512], "float32"), "b5": ("psum", [128, 512], "float32"),
    "b6": ("psum", [128, 512], "float32"), "b7": ("psum", [128, 512], "float32"),
}
_LAYERS = ["h", "u", "v"]
SEMAPHORES = (["ld_" + k for k in ("x", "w1", "w2", "pw", "px0", "px1")]
              + ["q_" + k for k in ("x", "w1", "w2", "pw", "px0", "px1")]
              + [p + k for k in _LAYERS for p in ("m0_", "m1_", "s_", "v_", "q_")]
              + ["m0_y", "m1_y", "s_y", "v_y", "m0_za", "m1_za", "m0_zb", "m1_zb", "s_z0", "v_z0", "s_z1", "v_z1"]
              + ["h_in", "w_in", "e_in", "l_in", "sent", "c_sent", "stored"])


def _engines(mask):
    return [1 << k for k in range(mask.bit_length()) if mask >> k & 1]


def _same_chip(topo, a, b):
    return topo.host(a) == topo.host(b) and topo.chip(a) == topo.chip(b)


def _shares(topo, src, dsts):
    off = [d for d in dsts if not _same_chip(topo, src, d)]
    on = [d for d in dsts if _same_chip(topo, src, d)]
    out = {}
    taken = 0
    for group in (off, on):
        if group:
            free = _engines(topo.mask(src, group[0]) & ~taken)
            each = 1 << ((len(free) // len(group)).bit_length() - 1)
            for k, d in enumerate(group):
                out[d] = sum(free[k * each:(k + 1) * each])
            taken |= sum(free)
    return out


def rank_program(g, core, T, topo):
    rank = T.rank_of(core)
    if rank is None:
        return
    S, cores = T.sem, T.cores
    n_ranks = len(cores)
    first, mid_e, mid_l, last = 0, 1, 2, n_ranks - 1
    E, L = (0, HALF), (HALF, COLS)

    def load(queue, buf, src, lo, hi, sem):
        queue.dma_start(buf[:, lo:hi], src[:, lo:hi]).then_inc(S[sem], 16)

    def pack(q, s, b, lo, hi, ld, sem):
        g.vector.wait_ge(S[ld], 16)
        g.vector.quantize_mx(q[:, lo:hi], s[:, lo:hi], b[:, 4 * lo:4 * hi]).then_inc(S[sem], 1)

    def layer(tag, waits, wq, ws, iq, isc, ilo, n, bank0, bank1, tb, tlo, oq, osc, olo):
        for sem, val in waits:
            g.tensor.wait_ge(S[sem], val)
        for i, bank in ((0, bank0), (1, bank1)):
            g.tensor.matmul_mx(bank[:, 0:n], wq[:, 128 * i:128 * i + 128], ws[:, 128 * i:128 * i + 128],
                               iq[:, ilo:ilo + n], isc[:, ilo:ilo + n], True, True).then_inc(S["m%d_%s" % (i, tag)], 1)
        lo, hi = 4 * tlo, 4 * (tlo + n)
        g.scalar.wait_ge(S["m0_" + tag], 1)
        g.vector.wait_ge(S["m1_" + tag], 1)
        for b, k in ((0, K), (1, -K)):
            g.scalar.activation(tb[:, lo + b:hi:4], bank0[:, 0:n], ActivationFunctionType.Relu,
                                scale=k).then_inc(S["s_" + tag], 1)
            g.vector.tensor_scalar(tb[:, lo + 2 + b:hi:4], bank1[:, 0:n], k, 0.0,
                                   AluOpType.mult, AluOpType.max).then_inc(S["v_" + tag], 1)
        g.vector.wait_ge(S["s_" + tag], 2)
        g.vector.wait_ge(S["v_" + tag], 2)
        g.vector.quantize_mx(oq[:, olo:olo + n], osc[:, olo:olo + n], tb[:, lo:hi]).then_inc(S["q_" + tag], 1)

    def views(q, s, lo, hi):
        return q[:, lo:hi].bitcast(dt.uint8), s[:, lo:hi]

    def count(mask):
        return len(_engines(mask))

    def send(dst, out, in_, mask, sem, local):
        rid, pid = topo.addr(cores[dst], core)
        g.remote_dma(out, in_, S[sem], S[local], pid, rid, mask)
        return count(mask)

    def send_pair(dst, dq, ds, sq, ss, lo, hi, masks, sem, local):
        n = 0
        for out, in_, mask in zip(views(dq, ds, lo, hi), views(sq, ss, lo, hi), masks):
            n += send(dst, out, in_, mask, sem, local)
        return n

    def send_fused(jobs, local):
        ts = []
        for dst, out, in_, mask, sem in jobs:
            rid, pid = topo.addr(cores[dst], core)
            ts.append(RemoteDMATransfer(dst_ids=[DstId(rid=rid, pnc=pid)], dma_engine_mask=mask, remote_sem=S[sem],
                                        src=in_, dst=out))
        g.remote_dma_fused(ts, local_sem=S[local])
        return sum(count(j[3]) for j in jobs)

    def full(src, dst):
        return topo.mask(cores[src], cores[dst])

    def both(src, dst):
        return full(src, dst), full(src, dst)

    def total(masks):
        return sum(count(m) for m in masks)

    def h_mask(src, dst):
        return _shares(topo, cores[src], [c for c in cores if c != cores[src]])[cores[dst]]

    def send_h():
        g.wait_ge(S.q_h, 1)
        lo, hi = 128 * rank, 128 * rank + 128
        n = 0
        for v in views(T.hq, T.hs, lo, hi):
            n += send_fused([(d, v, v, h_mask(rank, d), "h_in") for d in range(n_ranks) if d != rank], "sent")
        return n

    def make_h():
        pack(T.xq, T.xs, T.xb, 0, 128, "ld_x", "q_x")
        pack(T.w1q, T.w1s, T.w1b, 0, 256, "ld_w1", "q_w1")
        layer("h", [("q_x", 1), ("q_w1", 1)], T.w1q, T.w1s, T.xq, T.xs, 0, 128, T.b0, T.b1, T.hb, 0, T.hq, T.hs, 128 * rank)

    def make_y():
        arrivals = sum(2 * count(h_mask(s, rank)) for s in range(n_ranks) if s != rank)
        for sem, val in (("q_w2", 1), ("q_h", 1), ("h_in", arrivals)):
            g.tensor.wait_ge(S[sem], val)
        for k, bank in ((0, T.b6), (1, T.b7)):
            g.tensor.matmul_mx(bank[:, 0:256], T.w2q[:, 0:128], T.w2s[:, 0:128], T.hq[:, 256 * k:256 * k + 256],
                               T.hs[:, 256 * k:256 * k + 256], True, True).then_inc(S["m%d_y" % k], 1)
        g.scalar.wait_ge(S.m0_y, 1)
        g.scalar.activation(T.yb[:, 0:256], T.b6[:, 0:256], ActivationFunctionType.Copy).then_inc(S.s_y, 1)
        g.vector.wait_ge(S.m1_y, 1)
        g.vector.tensor_copy(T.yb[:, 256:512], T.b7[:, 0:256]).then_inc(S.v_y, 1)

    def store_y():
        g.sync.wait_ge(S.s_y, 1)
        g.sync.wait_ge(S.v_y, 1)
        g.sync.dma_start(T.y[:, :], T.yb[:, :]).then_inc(S.stored, 16)

    e_masks = full(first, mid_e), full(first, mid_e) & ~full(first, mid_l)
    l_masks = both(first, mid_l)
    PX = (E, L)
    m_px = full(last, first)
    sent = 0

    if rank == last:
        for k, (lo, hi) in enumerate(PX):
            load(g.sync, T.pxb, T.px, 4 * lo, 4 * hi, "ld_px%d" % k)
        load(g.sync, T.xb, T.x, 0, 512, "ld_x")
        load(g.sync, T.w1b, T.w1, 0, 1024, "ld_w1")
        for k, (lo, hi) in enumerate(PX):
            pack(T.pxq, T.pxs, T.pxb, lo, hi, "ld_px%d" % k, "q_px%d" % k)
        cd, cs = T.cq[:, E[0]:E[1]].bitcast(dt.uint8), T.pxq[:, E[0]:E[1]].bitcast(dt.uint8)
        g.wait_ge(S.q_px0, 1)
        px_sent = send(first, cd, cs, m_px, "e_in", "c_sent")
        g.wait_ge(S.q_px1, 1)
        px_sent += send(first, T.cs[:, 0:COLS], T.pxs[:, 0:COLS], m_px, "e_in", "c_sent")
        cd, cs = T.cq[:, L[0]:L[1]].bitcast(dt.uint8), T.pxq[:, L[0]:L[1]].bitcast(dt.uint8)
        px_sent += send(first, cd, cs, m_px, "l_in", "c_sent")
        make_h()
        sent += send_h()
        g.sync.wait_ge(S.c_sent, px_sent)
        load(g.sync, T.w2b, T.w2, 0, 512, "ld_w2")
        load(g.sync, T.pwb, T.pw, 0, 1024, "ld_pw")
        pack(T.w2q, T.w2s, T.w2b, 0, 128, "ld_w2", "q_w2")
        pack(T.pwq, T.pws, T.pwb, 0, 256, "ld_pw", "q_pw")
        make_y()
        store_y()
        g.tensor.wait_ge(S.q_pw, 1)
        for tag, (lo, hi), sem, src, banks in (("za", E, "e_in", mid_e, (T.b2, T.b3)), ("zb", L, "l_in", mid_l, (T.b4, T.b5))):
            g.tensor.wait_ge(S[sem], total(both(src, last)))
            for i in (0, 1):
                g.tensor.matmul_mx(banks[i][:, 0:HALF], T.pwq[:, 128 * i:128 * i + 128], T.pws[:, 128 * i:128 * i + 128],
                                   T.cq[:, lo:hi], T.cs[:, lo:hi], True, True).then_inc(S["m%d_%s" % (i, tag)], 1)
            g.scalar.wait_ge(S["m0_" + tag], 1)
            g.vector.wait_ge(S["m1_" + tag], 1)
            for blk in range(COLS // 128):
                c0, c1 = max(lo, 128 * blk), min(hi, 128 * blk + 128)
                if c0 >= c1:
                    continue
                done = "z0" if blk == 0 else "z1"
                for i, bank in enumerate(banks):
                    o = 128 * (2 * blk + i) + c0 - 128 * blk
                    out, in_ = T.zb[:, o:o + c1 - c0], bank[:, c0 - lo:c1 - lo]
                    if i == 0:
                        g.scalar.activation(out, in_, ActivationFunctionType.Copy).then_inc(S["s_" + done], 1)
                    else:
                        g.vector.tensor_copy(out, in_).then_inc(S["v_" + done], 1)
        g.sync.wait_ge(S.s_z0, 1)
        g.sync.wait_ge(S.v_z0, 1)
        g.sync.dma_start(T.z[:, 0:256], T.zb[:, 0:256]).then_inc(S.stored, 16)
        g.sync.wait_ge(S.s_z1, 3)
        g.sync.wait_ge(S.v_z1, 3)
        g.sync.dma_start(T.z[:, 256:768], T.zb[:, 256:768]).then_inc(S.stored, 16)
        g.sync.wait_ge(S.stored, 48)

    elif rank == first:
        load(g.sync, T.w1b, T.w1, 0, 1024, "ld_w1")
        load(g.scalar, T.xb, T.x, 0, 512, "ld_x")
        load(g.sync, T.pwb, T.pw, 0, 1024, "ld_pw")
        load(g.scalar, T.w2b, T.w2, 0, 512, "ld_w2")
        make_h()
        sent += send_h()
        pack(T.pwq, T.pws, T.pwb, 0, 256, "ld_pw", "q_pw")
        pack(T.w2q, T.w2s, T.w2b, 0, 128, "ld_w2", "q_w2")
        layer("u", [("q_pw", 1), ("e_in", 2 * count(m_px))], T.pwq, T.pws, T.cq, T.cs, E[0], HALF, T.b2, T.b3,
              T.t1b, E[0], T.t1q, T.t1s, E[0])
        layer("v", [("l_in", count(m_px))], T.pwq, T.pws, T.cq, T.cs, L[0], HALF, T.b4, T.b5,
              T.t1b, L[0], T.t1q, T.t1s, L[0])
        g.wait_ge(S.q_u, 1)
        c_sent = send_pair(mid_e, T.cq, T.cs, T.t1q, T.t1s, E[0], E[1], e_masks, "e_in", "c_sent")
        g.wait_ge(S.q_v, 1)
        c_sent += send_pair(mid_l, T.cq, T.cs, T.t1q, T.t1s, L[0], L[1], l_masks, "l_in", "c_sent")
        make_y()
        g.sync.wait_ge(S.c_sent, c_sent)
        store_y()
        g.sync.wait_ge(S.stored, 16)

    else:
        other = mid_l if rank == mid_e else mid_e
        (lo, hi), c_in, masks = (E, "e_in", e_masks) if rank == mid_e else (L, "l_in", l_masks)
        load(g.sync, T.pwb, T.pw, 0, 1024, "ld_pw")
        load(g.scalar, T.xb, T.x, 0, 512, "ld_x")
        load(g.sync, T.w1b, T.w1, 0, 1024, "ld_w1")
        load(g.scalar, T.w2b, T.w2, 0, 512, "ld_w2")
        pack(T.pwq, T.pws, T.pwb, 0, 256, "ld_pw", "q_pw")
        g.wait_ge(S.q_pw, 1)
        sent += send_pair(other, T.owq, T.ows, T.pwq, T.pws, 0, 256, both(rank, other), "w_in", "sent")
        make_h()
        sent += send_h()
        pack(T.w2q, T.w2s, T.w2b, 0, 128, "ld_w2", "q_w2")
        w_in = ("w_in", total(both(other, rank)))
        mine, theirs = (T.pwq, T.pws, ("q_pw", 1)), (T.owq, T.ows, w_in)
        s1, s2 = (mine, theirs) if rank < other else (theirs, mine)
        layer("u", [s1[2], (c_in, total(masks))], s1[0], s1[1], T.cq, T.cs, lo, HALF, T.b2, T.b3,
              T.t1b, lo, T.t1q, T.t1s, lo)
        layer("v", [s2[2], ("q_u", 1)], s2[0], s2[1], T.t1q, T.t1s, lo, HALF, T.b4, T.b5, T.t2b, lo, T.t2q, T.t2s, lo)
        g.wait_ge(S.q_v, 1)
        c_sent = send_pair(last, T.cq, T.cs, T.t2q, T.t2s, lo, hi, both(rank, last), c_in, "c_sent")
        make_y()
        g.sync.wait_ge(S.c_sent, c_sent)
        store_y()
        g.sync.wait_ge(S.stored, 16)

    g.wait_ge(S.sent, sent)
